import numpy as np
import ml_dtypes


def mxq(x, axis, fmt="e4m3"):
    dtype, down = {"e4m3": (ml_dtypes.float8_e4m3fn, 7), "e5m2": (ml_dtypes.float8_e5m2, 14)}[fmt]
    v = np.moveaxis(np.asarray(x, np.float32).astype(ml_dtypes.bfloat16).astype(np.float64), axis, -1)
    blocks = v.reshape(v.shape[:-1] + (-1, 32))
    amax = np.abs(blocks).max(-1, keepdims=True)
    byte = np.maximum(np.where(amax > 0, np.frexp(amax)[1] - 1 + 127, 0) - down, 1)
    scale = np.exp2(byte - 127.0)
    codes = (blocks / scale).astype(np.float32).astype(dtype).astype(np.float64)
    return np.moveaxis((codes * scale).reshape(v.shape), -1, axis)


WIDE = False


def mx_kscale(k):
    if not WIDE:
        return np.ones(k)
    levels = np.array([10, -10, 5, -5, 0])
    if k % 512:
        return np.exp2(np.random.permutation(np.resize(levels, k // 32))).repeat(32)
    a = np.empty((k // 512, 16))
    for p in range(k // 512):
        a[p, :8] = np.random.permutation(np.resize(levels, 8))
        for g in range(8):
            far = levels[np.abs(levels - a[p, g]) >= 10]
            a[p, g + 8] = far[np.random.randint(len(far))]
    return np.exp2(a.ravel()).repeat(32)


def f64(x):
    return np.asarray(x).astype(np.float64)


def striped(idx):
    return np.tile(idx.reshape(-1, 16).T, (8, 1)).astype(np.uint16)


def unstriped(offs):
    return offs[:16].T.reshape(-1).astype(np.int64)


def striped8(idx):
    return np.concatenate([x.reshape(-1, 16).T for x in idx]).astype(np.uint16)


def runs(offs, k):
    lists = np.stack([offs[16 * r : 16 * r + 16].T.reshape(-1) for r in range(8)]).astype(np.int64)
    return lists[np.arange(k) % 512 // 64]


def pack_weight(w):
    k, n = w.shape
    w = f64(np.asarray(w, np.float32).astype(ml_dtypes.bfloat16)).reshape(k // 32, 32, n)
    amax = np.abs(w).max(1)
    byte = np.clip(np.where(amax > 0, np.frexp(amax)[1] - 1 + 127 - 7, 1), 1, 254)
    scaled = (w * np.exp2(127.0 - byte)[:, None, :]).reshape(k, n).astype(np.float32)
    words = np.ascontiguousarray(scaled.reshape(k // 512, 128, 4, n).transpose(0, 1, 3, 2)).astype(ml_dtypes.float8_e4m3fn).view(np.uint8)
    return words, np.ascontiguousarray(byte.astype(np.uint8).reshape(k // 512, 16, n))


def unpack_weight(words, scales):
    g, p, n, _ = words.shape
    vals = np.ascontiguousarray(words).view(ml_dtypes.float8_e4m3fn).astype(np.float64) * np.repeat(np.exp2(scales.astype(np.float64) - 127.0), 8, axis=1)[..., None]
    return vals.transpose(0, 1, 3, 2).reshape(g * 512, n)


E2M1 = np.array([0.0, 0.5, 1.0, 1.5, 2.0, 3.0, 4.0, 6.0, -0.0, -0.5, -1.0, -1.5, -2.0, -3.0, -4.0, -6.0])


def pack_fp4(w):
    k, n = w.shape
    w = f64(np.asarray(w, np.float32).astype(ml_dtypes.bfloat16)).reshape(k // 32, 32, n)
    amax = np.abs(w).max(1)
    mant, ex = np.frexp(amax / 6.0)
    byte = np.clip(np.where(amax > 0, np.where(mant > 0.5, ex, ex - 1) + 127, 1), 1, 254)
    scaled = (w * np.exp2(127.0 - byte)[:, None, :]).reshape(k, n).astype(np.float32)
    c = np.ascontiguousarray(scaled.reshape(k // 512, 128, 4, n).transpose(0, 1, 3, 2)).astype(ml_dtypes.float4_e2m1fn).view(np.uint8) & 0xF
    words = (c[..., 0::2] | (c[..., 1::2] << 4)).reshape(k // 512, 128, 2 * n)
    return np.ascontiguousarray(words), np.ascontiguousarray(byte.astype(np.uint8).reshape(k // 512, 16, n))


def unpack_fp4(words, scales):
    g, _, n = scales.shape
    words = np.ascontiguousarray(words).reshape(g, 128, n, 2)
    nib = np.empty((g, 128, n, 4), np.uint8)
    nib[..., 0::2] = words & 0xF
    nib[..., 1::2] = words >> 4
    vals = E2M1[nib] * np.repeat(np.exp2(scales.astype(np.float64) - 127.0), 8, axis=1)[..., None]
    return vals.transpose(0, 1, 3, 2).reshape(g * 512, n)


def planes(y):
    n, m = y.shape
    v = y.astype(np.float32).astype(ml_dtypes.bfloat16).astype(np.float64).reshape(n // 32, 32, m)
    top = np.abs(v).max(1)
    byte = np.clip(np.where(top > 0, np.frexp(top)[1] - 1 + 127 - 7, 1), 1, 254)
    codes = (v * np.exp2(127.0 - byte)[:, None, :]).reshape(n, m).astype(np.float32).astype(ml_dtypes.float8_e4m3fn).view(np.uint8)
    words = codes.reshape(n // 512, 128, 4, m).transpose(0, 1, 3, 2)
    return np.ascontiguousarray(words), np.ascontiguousarray(byte.astype(np.uint8).reshape(n // 512, 16, m))


K, T, S, N, H, C = 512, 2048, 256, 512, 512, 512


def setup_inputs():
    n = np.random.standard_normal
    s = mx_kscale(K)[:, None]
    u = mx_kscale(K)
    packed_xT = pack_weight(n((K, T)) * s)
    packed_w1 = pack_fp4(n((K, H)) / np.sqrt(K) / s)
    packed_w2 = pack_fp4(n((H, N)) / np.sqrt(H) / u[:, None])
    return {
        "x_words": packed_xT[0],
        "x_scales": packed_xT[1],
        "w1_words": packed_w1[0],
        "w1_scales": packed_w1[1],
        "gn": (np.random.uniform(0.5, 1.5, (H, 1)) * u[:, None]).astype(np.float32),
        "w2_words": packed_w2[0],
        "w2_scales": packed_w2[1],
        "gs": (np.random.uniform(0.5, 1.5, (K, 1)) / s).astype(np.float32),
        "offs": striped(np.random.permutation(T)[:S]),
        "n1": striped(np.random.permutation(S)),
        "n2": striped(np.random.permutation(S)),
        "n3": striped8(np.stack([np.random.permutation(S) for _ in range(8)])),
        "n4": striped8(np.stack([np.random.permutation(S) for _ in range(8)])),
        "n5": striped8(np.stack([np.random.permutation(S) for _ in range(8)])),
        "cand": striped(np.random.permutation(T)[:C]),
        "n6": striped(np.random.permutation(S)),
        "n7": striped(np.random.permutation(S)),
    }


def reference(x_words, x_scales, w1_words, w1_scales, gn, w2_words, w2_scales, gs, offs, n1, n2, n3, n4, n5, cand, n6, n7):
    xq = unpack_weight(x_words, x_scales)[:, unstriped(offs)]
    y = unpack_fp4(w1_words, w1_scales).T @ xq
    pa = y[:, unstriped(n1)]
    pb = y[:, unstriped(n2)]
    mu = 0.3125 * (y + pa + pb)
    z = f64(gn) * ((y - mu) / (np.sqrt((pa - mu) ** 2 + (pb - mu) ** 2 + 0.25)))
    a = unpack_fp4(w2_words, w2_scales).T @ mxq(z, 0, "e4m3")
    x_cand = unpack_weight(x_words, x_scales)[:, unstriped(cand)]
    z2 = f64(gs) * (np.maximum(y, y[np.arange(H)[:, None], runs(n3, H)]) - (np.maximum(y[np.arange(H)[:, None], runs(n4, H)], y[np.arange(H)[:, None], runs(n5, H)])))
    b = 0.0625 * ((x_cand.T @ mxq(z2, 0, "e4m3")))
    out_0 = a * (np.tanh(b[:, unstriped(n6)] - b[:, unstriped(n7)]))
    return (out_0,) + planes(out_0)

@@ -1,0 +1,312 @@
+from contextlib import ExitStack
+
+import concourse.mybir as mybir
+
+K, T, S, C = 512, 2048, 256, 512
+FLOPS = 3 * 2 * 512 * 512 * 256
+
+F32 = mybir.dt.float32
+BF16 = mybir.dt.bfloat16
+I32 = mybir.dt.int32
+U32 = mybir.dt.uint32
+U16 = mybir.dt.uint16
+U8 = mybir.dt.uint8
+FP8X4 = mybir.dt.float8_e4m3fn_x4
+FP4X4 = mybir.dt.float4_e2m1fn_x4
+ALU = mybir.AluOpType
+ACT = mybir.ActivationFunctionType
+
+P = 128
+PACK = 4
+WINDOW = 2 * S
+
+
+def load_scale_rows(queue, tile, rows):
+    for q in range(4):
+        queue.dma_start(out=tile[32 * q : 32 * q + 4, :].bitcast(I32), in_=rows[0, 4 * q : 4 * q + 4, :].bitcast(I32))
+
+
+def interleave(nc, grouped, planes, cols):
+    nc.vector.tensor_copy(
+        out=grouped[:, cols, :].rearrange("p (c i) t -> p c t i", i=4),
+        in_=planes[:, :, cols].rearrange("p t (c i) -> p c t i", i=4),
+    )
+
+
+def quantize(nc, codes, scales, grouped, cols):
+    nc.vector.quantize_mx(
+        out=codes[:, cols].bitcast(FP8X4), scales=scales[:, cols], in_=grouped[:, cols, :].rearrange("p j t -> p (j t)")
+    )
+
+
+def tile_picked_fkcdjointbstdmix_none_po_kernel(
+    tc, x_words, x_scales, w1_words, w1_scales, gn, w2_words, w2_scales, gs,
+    offs, n1, n2, n3, n4, n5, cand, n6, n7, out_0, out_1, out_2,
+):
+    nc = tc.nc
+    with ExitStack() as ctx:
+        keep = ctx.enter_context(tc.tile_pool(name="keep", bufs=1))
+        psum = ctx.enter_context(tc.psum_pool(name="psum", bufs=1))
+
+        def sb(name, shape, dtype):
+            return keep.tile(shape, dtype, name=name, align_bytes=64)
+
+        lists = {}
+        for name, src in (("offs", offs), ("n1", n1), ("n2", n2), ("n3", n3), ("n4", n4), ("n5", n5),
+                          ("cand", cand), ("n6", n6), ("n7", n7)):
+            lists[name] = (sb("list_" + name, list(src.shape), U16), src)
+
+        def load_list(name):
+            nc.sync.dma_start(lists[name][0][:], lists[name][1])
+
+        def offsets(name):
+            return lists[name][0][:]
+
+        xw = sb("xw", [P, T], I32)
+        xs = sb("xs", [P, T], U8)
+        w1w = sb("w1w", [P, 2 * K], U8)
+        w1s = sb("w1s", [P, K], U8)
+        w2w = sb("w2w", [P, 2 * K], U8)
+        w2s = sb("w2s", [P, K], U8)
+        gn_sb = sb("gn_sb", [P, PACK], F32)
+        gs_sb = sb("gs_sb", [P, PACK], F32)
+        win = [sb("win%d" % t, [P, WINDOW], F32) for t in range(PACK)]
+
+        nc.gpsimd.memset(xs[:].bitcast(I32), 0)
+        nc.vector.memset(w1s[:].bitcast(I32), 0)
+        nc.vector.memset(w2s[:].bitcast(I32), 0)
+        for t in range(PACK):
+            nc.gpsimd.memset(win[t][:, S:], 0.0)
+
+        load_list("offs")
+        nc.sync.dma_start(out=w1w[:].bitcast(I32), in_=w1_words[0].bitcast(I32))
+        nc.sync.dma_start(out=xw[:], in_=x_words[0].rearrange("p n t -> p (n t)").bitcast(I32))
+        load_scale_rows(nc.sync, w1s, w1_scales)
+        load_scale_rows(nc.sync, xs, x_scales)
+        load_list("cand")
+        load_list("n1")
+        load_list("n2")
+        load_list("n3")
+        load_list("n4")
+        load_list("n5")
+        nc.sync.dma_start(out=w2w[:].bitcast(I32), in_=w2_words[0].bitcast(I32))
+        load_scale_rows(nc.sync, w2s, w2_scales)
+        nc.sync.dma_start(out=gs_sb[:], in_=gs.rearrange("(p t) o -> p (t o)", t=PACK))
+        nc.sync.dma_start(out=gn_sb[:], in_=gn.rearrange("(p t) o -> p (t o)", t=PACK))
+        load_list("n6")
+        load_list("n7")
+
+        def deal_fp4(engine, name, words, scales):
+            dw = sb(name + "_dw", [P, 2 * K], U8)
+            ds = sb(name + "_ds", [P, K], U8)
+            engine.tensor_copy(
+                out=dw[:].rearrange("p (t m b) -> p t m b", t=PACK, b=2),
+                in_=words[:].rearrange("p (m t b) -> p t m b", t=PACK, b=2),
+            )
+            engine.tensor_copy(
+                out=ds[:].rearrange("p (t m) -> p t m", t=PACK),
+                in_=scales[:].rearrange("p (m t) -> p t m", t=PACK),
+            )
+            return dw, ds
+
+        w1_dw, w1_ds = deal_fp4(nc.vector, "w1", w1w, w1s)
+
+        xq_w = sb("xq_w", [P, S], U32)
+        xq_s = sb("xq_s", [P, S], U8)
+        xc_w = sb("xc_w", [P, C], U32)
+        xc_s = sb("xc_s", [P, C], U8)
+        xd_w = sb("xd_w", [P, C], U32)
+        xd_s = sb("xd_s", [P, C], U8)
+        nc.vector.tensor_copy(xq_s[:], xs[:].indirect(offsets("offs")))
+        nc.vector.tensor_copy(xq_w[:], xw[:].bitcast(U32).indirect(offsets("offs")))
+
+        y_ps = [psum.tile([P, S], F32, name="y_ps%d" % t, tag="low%d" % t) for t in range(PACK)]
+        for t in range(PACK):
+            nc.tensor.matmul_mx(
+                out=y_ps[t][:],
+                lhsT=w1_dw[:, 2 * P * t : 2 * P * (t + 1)].bitcast(FP4X4),
+                lhsT_scale=w1_ds[:, P * t : P * (t + 1)],
+                rhs=xq_w[:].bitcast(FP8X4),
+                rhs_scale=xq_s[:],
+                start=True,
+                stop=True,
+            )
+
+        nc.vector.tensor_copy(xc_s[:], xs[:].indirect(offsets("cand")))
+        nc.vector.tensor_copy(xc_w[:], xw[:].bitcast(U32).indirect(offsets("cand")))
+        nc.vector.tensor_copy(
+            out=xd_s[:].rearrange("p (t m) -> p t m", t=PACK), in_=xc_s[:].rearrange("p (m t) -> p t m", t=PACK)
+        )
+        nc.vector.tensor_copy(
+            out=xd_w[:].rearrange("p (t m) -> p t m", t=PACK), in_=xc_w[:].rearrange("p (m t) -> p t m", t=PACK)
+        )
+        w2_dw, w2_ds = deal_fp4(nc.gpsimd, "w2", w2w, w2s)
+        gn_scaled = sb("gn_scaled", [P, PACK], F32)
+        nc.gpsimd.tensor_scalar(gn_scaled[:], gn_sb[:], 0.6875, 0.0, ALU.mult, ALU.add)
+
+        pa = sb("pa", [P, PACK, S], F32)
+        for t in range(PACK):
+            nc.scalar.copy(win[t][:, :S], y_ps[t][:])
+            nc.scalar.activation(pa[:, t, :], win[t][:].indirect(offsets("n1")), ACT.Copy)
+
+        u = sb("u", [P, PACK, S], F32)
+        ev = sb("ev", [P, 2, 2, 2, S], F32)
+        dev = sb("dev", [P, PACK, S], F32)
+
+        def pair_sum(t):
+            nc.vector.tensor_tensor(u[:, t, :], win[t][:].indirect(offsets("n2")), pa[:, t, :], ALU.add)
+
+        def spreads(t):
+            nc.vector.scalar_tensor_tensor(ev[:, t // 2, 1, t % 2, :], pa[:, t, :], -2.0, u[:, t, :], ALU.mult, ALU.add)
+            nc.vector.scalar_tensor_tensor(ev[:, t // 2, 0, t % 2, :], u[:, t, :], 0.6, y_ps[t][:], ALU.mult, ALU.subtract)
+
+        def deviation(t):
+            nc.vector.scalar_tensor_tensor(dev[:, t, :], u[:, t, :], -5.0 / 11.0, y_ps[t][:], ALU.mult, ALU.add)
+
+        pair_sum(0)
+        pair_sum(1)
+        spreads(0)
+        pair_sum(2)
+        spreads(1)
+        pair_sum(3)
+        spreads(2)
+        spreads(3)
+
+        early = sb("early", [P, 2, 3, S], F32)
+        fetched = [[early[:, t, k, :] for k in range(3)] for t in range(2)]
+        fetched = fetched + [[ev[:, h, k // 2, k % 2, :] for k in range(3)] for h in range(2)]
+        m1 = sb("m1", [P, PACK, S], F32)
+        m2 = sb("m2", [P, PACK, S], F32)
+        dm = sb("dm", [P, PACK, S], F32)
+        z2_planes = sb("z2_planes", [P, PACK, S], BF16)
+
+        def group_gathers(t):
+            for k, name in enumerate(("n3", "n4", "n5")):
+                nc.scalar.activation(fetched[t][k], win[t][:].indirect(offsets(name)), ACT.Copy)
+
+        def maxima(t):
+            nc.vector.tensor_tensor(m1[:, t, :], fetched[t][0], y_ps[t][:], ALU.max)
+            nc.vector.tensor_tensor(m2[:, t, :], fetched[t][1], fetched[t][2], ALU.max)
+
+        def max_difference(t, cols):
+            nc.vector.tensor_tensor(dm[:, t, cols], m1[:, t, cols], m2[:, t, cols], ALU.subtract)
+
+        def z2_round(t, cols):
+            nc.vector.tensor_scalar(z2_planes[:, t, cols], dm[:, t, cols], gs_sb[:, t : t + 1], None, ALU.mult)
+
+        sq = sb("sq", [P, 2, 2, 2 * S], F32)
+        q = sb("q", [P, 2, 2 * S], F32)
+        r = sb("r", [P, PACK, S], F32)
+
+        def squares(h):
+            nc.scalar.activation(
+                sq[:, h].rearrange("p k n -> p (k n)"), ev[:, h].rearrange("p k t n -> p (k t n)"), ACT.Square
+            )
+
+        def square_sum(h):
+            nc.vector.scalar_tensor_tensor(q[:, h, :], sq[:, h, 0, :], 0.390625, sq[:, h, 1, :], ALU.mult, ALU.add)
+
+        whole = slice(0, S)
+        halves = [slice(0, S // 2), slice(S // 2, S)]
+        group_gathers(0)
+        group_gathers(1)
+        squares(0)
+        group_gathers(2)
+        squares(1)
+        group_gathers(3)
+        for t in range(3):
+            maxima(t)
+            deviation(t)
+            max_difference(t, whole)
+            if t > 0:
+                square_sum(t - 1)
+            else:
+                deviation(3)
+            z2_round(t, whole)
+        nc.scalar.activation(
+            r[:].rearrange("p t n -> p (t n)"), q[:].rearrange("p h n -> p (h n)"), ACT.Abs_reciprocal_sqrt,
+            bias=0.25, scale=0.5,
+        )
+
+        z2_grouped = sb("z2_grouped", [P, S, PACK], BF16)
+        z2_w = sb("z2_w", [P, S], U32)
+        z2_s = sb("z2_s", [P, S], U8)
+        maxima(3)
+        for cols in halves:
+            max_difference(3, cols)
+        for cols in halves:
+            z2_round(3, cols)
+        for cols in halves:
+            interleave(nc, z2_grouped, z2_planes, cols)
+        for cols in halves:
+            quantize(nc, z2_w, z2_s, z2_grouped, cols)
+
+        b_ps = [psum.tile([P, S], F32, name="b_ps%d" % t, tag="high%d" % t) for t in range(PACK)]
+        for t in range(PACK):
+            nc.tensor.matmul_mx(
+                out=b_ps[t][:],
+                lhsT=xd_w[:, P * t : P * (t + 1)].bitcast(FP8X4),
+                lhsT_scale=xd_s[:, P * t : P * (t + 1)],
+                rhs=z2_w[:].bitcast(FP8X4),
+                rhs_scale=z2_s[:],
+                start=True,
+                stop=True,
+            )
+
+        z_planes = sb("z_planes", [P, PACK, S], BF16)
+        z_grouped = sb("z_grouped", [P, S, PACK], BF16)
+        z_w = sb("z_w", [P, S], U32)
+        z_s = sb("z_s", [P, S], U8)
+        for t in range(PACK):
+            nc.vector.scalar_tensor_tensor(
+                z_planes[:, t, :], dev[:, t, :], gn_scaled[:, t : t + 1], r[:, t, :], ALU.mult, ALU.mult
+            )
+        for cols in halves:
+            interleave(nc, z_grouped, z_planes, cols)
+        for cols in halves:
+            quantize(nc, z_w, z_s, z_grouped, cols)
+
+        a_ps = [psum.tile([P, S], F32, name="a_ps%d" % t, tag="low%d" % t) for t in range(PACK)]
+        for t in range(PACK):
+            nc.tensor.matmul_mx(
+                out=a_ps[t][:],
+                lhsT=w2_dw[:, 2 * P * t : 2 * P * (t + 1)].bitcast(FP4X4),
+                lhsT_scale=w2_ds[:, P * t : P * (t + 1)],
+                rhs=z_w[:].bitcast(FP8X4),
+                rhs_scale=z_s[:],
+                start=True,
+                stop=True,
+            )
+
+        b6 = sb("b6", [P, PACK, S], F32)
+        diff = sb("diff", [P, PACK, S], F32)
+        gate = sb("gate", [P, PACK, S], F32)
+        res = sb("res", [P, PACK, S], F32)
+        out_rows = out_0.rearrange("(p t) j -> p t j", t=PACK)
+
+        def finish(t):
+            nc.scalar.activation(gate[:, t, :], diff[:, t, :], ACT.Tanh, scale=-0.0625)
+            nc.vector.tensor_tensor(res[:, t, :], gate[:, t, :], a_ps[t][:], ALU.mult)
+            nc.sync.dma_start(out=out_rows[:, t, :], in_=res[:, t, :])
+
+        for t in range(PACK):
+            nc.scalar.copy(win[t][:, :S], b_ps[t][:])
+            nc.scalar.activation(b6[:, t, :], win[t][:].indirect(offsets("n6")), ACT.Copy)
+            nc.vector.tensor_tensor(diff[:, t, :], win[t][:].indirect(offsets("n7")), b6[:, t, :], ALU.subtract)
+            if t > 0:
+                finish(t - 1)
+        finish(PACK - 1)
+
+        o_grouped = sb("o_grouped", [P, S, PACK], BF16)
+        o_w = sb("o_w", [P, S], I32)
+        o_s = sb("o_s", [P, S], U8)
+        for cols in halves:
+            interleave(nc, o_grouped, res, cols)
+        for cols in halves:
+            quantize(nc, o_w, o_s, o_grouped, cols)
+        nc.sync.dma_start(out=out_1[0].rearrange("p n t -> p (n t)").bitcast(I32), in_=o_w[:])
+        for k in range(4):
+            queue = nc.scalar if k % 2 == 0 else nc.sync
+            queue.dma_start(
+                out=out_2[0, 4 * k : 4 * k + 4, :].bitcast(I32), in_=o_s[32 * k : 32 * k + 4, :].bitcast(I32)
+            )

@@ -21,8 +21,8 @@ PACK = 4
 WINDOW = 2 * S
 
 
-def load_scale_rows(queue, tile, rows):
-    for q in range(4):
+def load_scale_rows(queues, tile, rows):
+    for q, queue in enumerate(queues):
         queue.dma_start(out=tile[32 * q : 32 * q + 4, :].bitcast(I32), in_=rows[0, 4 * q : 4 * q + 4, :].bitcast(I32))
 
 
@@ -48,8 +48,8 @@ def tile_picked_fkcdjointbstdmix_none_po_kernel(
         keep = ctx.enter_context(tc.tile_pool(name="keep", bufs=1))
         psum = ctx.enter_context(tc.psum_pool(name="psum", bufs=1))
 
-        def sb(name, shape, dtype):
-            return keep.tile(shape, dtype, name=name, align_bytes=64)
+        def sb(name, shape, dtype, tag=None):
+            return keep.tile(shape, dtype, name=name, tag=tag or name, align_bytes=64)
 
         lists = {}
         for name, src in (("offs", offs), ("n1", n1), ("n2", n2), ("n3", n3), ("n4", n4), ("n5", n5),
@@ -59,8 +59,10 @@ def tile_picked_fkcdjointbstdmix_none_po_kernel(
         def load_list(name):
             nc.sync.dma_start(lists[name][0][:], lists[name][1])
 
-        def offsets(name):
-            return lists[name][0][:]
+        def offsets(name, cols=slice(0, S)):
+            if name == "cand":
+                return lists[name][0][:]
+            return lists[name][0][:, cols.start // 16 : cols.stop // 16]
 
         xw = sb("xw", [P, T], I32)
         xs = sb("xs", [P, T], U8)
@@ -72,51 +74,58 @@ def tile_picked_fkcdjointbstdmix_none_po_kernel(
         gs_sb = sb("gs_sb", [P, PACK], F32)
         win = [sb("win%d" % t, [P, WINDOW], F32) for t in range(PACK)]
 
-        nc.gpsimd.memset(xs[:].bitcast(I32), 0)
-        nc.vector.memset(w1s[:].bitcast(I32), 0)
-        nc.vector.memset(w2s[:].bitcast(I32), 0)
+        nc.gpsimd.memset(w1s[:].bitcast(I32), 0)
+        nc.vector.memset(xs[:].bitcast(I32), 0)
         for t in range(PACK):
-            nc.gpsimd.memset(win[t][:, S:], 0.0)
+            nc.vector.memset(win[t][:, S:], 0.0)
+        nc.vector.memset(w2s[:].bitcast(I32), 0)
 
         load_list("offs")
+        load_list("cand")
         nc.sync.dma_start(out=w1w[:].bitcast(I32), in_=w1_words[0].bitcast(I32))
         nc.sync.dma_start(out=xw[:], in_=x_words[0].rearrange("p n t -> p (n t)").bitcast(I32))
-        load_scale_rows(nc.sync, w1s, w1_scales)
-        load_scale_rows(nc.sync, xs, x_scales)
-        load_list("cand")
+        load_scale_rows([nc.scalar] * 4, xs, x_scales)
+        load_scale_rows([nc.gpsimd, nc.gpsimd, nc.scalar, nc.scalar], w1s, w1_scales)
+        nc.gpsimd.dma_start(out=w2w[:].bitcast(I32), in_=w2_words[0].bitcast(I32))
         load_list("n1")
         load_list("n2")
         load_list("n3")
         load_list("n4")
         load_list("n5")
-        nc.sync.dma_start(out=w2w[:].bitcast(I32), in_=w2_words[0].bitcast(I32))
-        load_scale_rows(nc.sync, w2s, w2_scales)
+        load_scale_rows([nc.sync] * 4, w2s, w2_scales)
         nc.sync.dma_start(out=gs_sb[:], in_=gs.rearrange("(p t) o -> p (t o)", t=PACK))
         nc.sync.dma_start(out=gn_sb[:], in_=gn.rearrange("(p t) o -> p (t o)", t=PACK))
         load_list("n6")
         load_list("n7")
 
-        def deal_fp4(engine, name, words, scales):
-            dw = sb(name + "_dw", [P, 2 * K], U8)
-            ds = sb(name + "_ds", [P, K], U8)
-            engine.tensor_copy(
-                out=dw[:].rearrange("p (t m b) -> p t m b", t=PACK, b=2),
-                in_=words[:].rearrange("p (m t b) -> p t m b", t=PACK, b=2),
-            )
-            engine.tensor_copy(
-                out=ds[:].rearrange("p (t m) -> p t m", t=PACK),
-                in_=scales[:].rearrange("p (m t) -> p t m", t=PACK),
-            )
-            return dw, ds
+        unused = sb("unused", [P, 2], F32)
+        nc.scalar.activation(
+            unused[:, 0:1], win[0][:, S : S + 1], ACT.Abs_reciprocal_sqrt, bias=0.25, scale=0.5
+        )
 
-        w1_dw, w1_ds = deal_fp4(nc.vector, "w1", w1w, w1s)
+        def deal_words(name, words):
+            dealt = sb(name, [P, 2 * K], U8)
+            nc.scalar.copy(
+                out=dealt[:].bitcast(U16).rearrange("p (t m) -> p t m", t=PACK),
+                in_=words[:].bitcast(U16).rearrange("p (m t) -> p t m", t=PACK),
+            )
+            return dealt
+
+        def deal(name, columns, dtype):
+            dealt = sb(name, [P, K], dtype)
+            nc.vector.tensor_copy(
+                out=dealt[:].rearrange("p (t m) -> p t m", t=PACK),
+                in_=columns[:].rearrange("p (m t) -> p t m", t=PACK),
+            )
+            return dealt
+
+        w1_dw = deal_words("w1_dw", w1w)
+        w1_ds = deal("w1_ds", w1s, U8)
 
         xq_w = sb("xq_w", [P, S], U32)
         xq_s = sb("xq_s", [P, S], U8)
-        xc_w = sb("xc_w", [P, C], U32)
-        xc_s = sb("xc_s", [P, C], U8)
-        xd_w = sb("xd_w", [P, C], U32)
-        xd_s = sb("xd_s", [P, C], U8)
+        xc_w = sb("xc_w", [P, C], U32, tag="w1s")
+        xc_s = sb("xc_s", [P, C], U8, tag="xq_s")
         nc.vector.tensor_copy(xq_s[:], xs[:].indirect(offsets("offs")))
         nc.vector.tensor_copy(xq_w[:], xw[:].bitcast(U32).indirect(offsets("offs")))
 
@@ -132,15 +141,12 @@ def tile_picked_fkcdjointbstdmix_none_po_kernel(
                 stop=True,
             )
 
-        nc.vector.tensor_copy(xc_s[:], xs[:].indirect(offsets("cand")))
+        w2_dw = deal_words("w2_dw", w2w)
         nc.vector.tensor_copy(xc_w[:], xw[:].bitcast(U32).indirect(offsets("cand")))
-        nc.vector.tensor_copy(
-            out=xd_s[:].rearrange("p (t m) -> p t m", t=PACK), in_=xc_s[:].rearrange("p (m t) -> p t m", t=PACK)
-        )
-        nc.vector.tensor_copy(
-            out=xd_w[:].rearrange("p (t m) -> p t m", t=PACK), in_=xc_w[:].rearrange("p (m t) -> p t m", t=PACK)
-        )
-        w2_dw, w2_ds = deal_fp4(nc.gpsimd, "w2", w2w, w2s)
+        nc.vector.tensor_copy(xc_s[:], xs[:].indirect(offsets("cand")))
+        xd_w = deal("xd_w", xc_w, U32)
+        xd_s = deal("xd_s", xc_s, U8)
+        w2_ds = deal("w2_ds", w2s, U8)
         gn_scaled = sb("gn_scaled", [P, PACK], F32)
         nc.gpsimd.tensor_scalar(gn_scaled[:], gn_sb[:], 0.6875, 0.0, ALU.mult, ALU.add)
 
@@ -180,13 +186,13 @@ def tile_picked_fkcdjointbstdmix_none_po_kernel(
         dm = sb("dm", [P, PACK, S], F32)
         z2_planes = sb("z2_planes", [P, PACK, S], BF16)
 
-        def group_gathers(t):
+        def group_gathers(t, cols):
             for k, name in enumerate(("n3", "n4", "n5")):
-                nc.scalar.activation(fetched[t][k], win[t][:].indirect(offsets(name)), ACT.Copy)
+                nc.scalar.activation(fetched[t][k][:, cols], win[t][:].indirect(offsets(name, cols)), ACT.Copy)
 
-        def maxima(t):
-            nc.vector.tensor_tensor(m1[:, t, :], fetched[t][0], y_ps[t][:], ALU.max)
-            nc.vector.tensor_tensor(m2[:, t, :], fetched[t][1], fetched[t][2], ALU.max)
+        def maxima(t, cols):
+            nc.vector.tensor_tensor(m1[:, t, cols], fetched[t][0][:, cols], y_ps[t][:, cols], ALU.max)
+            nc.vector.tensor_tensor(m2[:, t, cols], fetched[t][1][:, cols], fetched[t][2][:, cols], ALU.max)
 
         def max_difference(t, cols):
             nc.vector.tensor_tensor(dm[:, t, cols], m1[:, t, cols], m2[:, t, cols], ALU.subtract)
@@ -208,14 +214,15 @@ def tile_picked_fkcdjointbstdmix_none_po_kernel(
 
         whole = slice(0, S)
         halves = [slice(0, S // 2), slice(S // 2, S)]
-        group_gathers(0)
-        group_gathers(1)
+        group_gathers(0, whole)
+        group_gathers(1, whole)
         squares(0)
-        group_gathers(2)
+        group_gathers(2, whole)
         squares(1)
-        group_gathers(3)
+        for cols in halves:
+            group_gathers(3, cols)
         for t in range(3):
-            maxima(t)
+            maxima(t, whole)
             deviation(t)
             max_difference(t, whole)
             if t > 0:
@@ -228,30 +235,28 @@ def tile_picked_fkcdjointbstdmix_none_po_kernel(
             bias=0.25, scale=0.5,
         )
 
+        nc.scalar.activation(unused[:, 1:2], r[:, 0, 0:1], ACT.Tanh)
+
         z2_grouped = sb("z2_grouped", [P, S, PACK], BF16)
         z2_w = sb("z2_w", [P, S], U32)
         z2_s = sb("z2_s", [P, S], U8)
-        maxima(3)
-        for cols in halves:
-            max_difference(3, cols)
-        for cols in halves:
-            z2_round(3, cols)
-        for cols in halves:
-            interleave(nc, z2_grouped, z2_planes, cols)
-        for cols in halves:
-            quantize(nc, z2_w, z2_s, z2_grouped, cols)
-
         b_ps = [psum.tile([P, S], F32, name="b_ps%d" % t, tag="high%d" % t) for t in range(PACK)]
-        for t in range(PACK):
-            nc.tensor.matmul_mx(
-                out=b_ps[t][:],
-                lhsT=xd_w[:, P * t : P * (t + 1)].bitcast(FP8X4),
-                lhsT_scale=xd_s[:, P * t : P * (t + 1)],
-                rhs=z2_w[:].bitcast(FP8X4),
-                rhs_scale=z2_s[:],
-                start=True,
-                stop=True,
-            )
+        for cols in halves:
+            maxima(3, cols)
+            max_difference(3, cols)
+            z2_round(3, cols)
+            interleave(nc, z2_grouped, z2_planes, cols)
+            quantize(nc, z2_w, z2_s, z2_grouped, cols)
+            for t in range(PACK):
+                nc.tensor.matmul_mx(
+                    out=b_ps[t][:, cols],
+                    lhsT=xd_w[:, P * t : P * (t + 1)].bitcast(FP8X4),
+                    lhsT_scale=xd_s[:, P * t : P * (t + 1)],
+                    rhs=z2_w[:, cols].bitcast(FP8X4),
+                    rhs_scale=z2_s[:, cols],
+                    start=True,
+                    stop=True,
+                )
 
         z_planes = sb("z_planes", [P, PACK, S], BF16)
         z_grouped = sb("z_grouped", [P, S, PACK], BF16)
@@ -284,26 +289,42 @@ def tile_picked_fkcdjointbstdmix_none_po_kernel(
         res = sb("res", [P, PACK, S], F32)
         out_rows = out_0.rearrange("(p t) j -> p t j", t=PACK)
 
-        def finish(t):
-            nc.scalar.activation(gate[:, t, :], diff[:, t, :], ACT.Tanh, scale=-0.0625)
-            nc.vector.tensor_tensor(res[:, t, :], gate[:, t, :], a_ps[t][:], ALU.mult)
-            nc.sync.dma_start(out=out_rows[:, t, :], in_=res[:, t, :])
-
-        for t in range(PACK):
-            nc.scalar.copy(win[t][:, :S], b_ps[t][:])
-            nc.scalar.activation(b6[:, t, :], win[t][:].indirect(offsets("n6")), ACT.Copy)
-            nc.vector.tensor_tensor(diff[:, t, :], win[t][:].indirect(offsets("n7")), b6[:, t, :], ALU.subtract)
-            if t > 0:
-                finish(t - 1)
-        finish(PACK - 1)
-
         o_grouped = sb("o_grouped", [P, S, PACK], BF16)
         o_w = sb("o_w", [P, S], I32)
         o_s = sb("o_s", [P, S], U8)
-        for cols in halves:
-            interleave(nc, o_grouped, res, cols)
-        for cols in halves:
-            quantize(nc, o_w, o_s, o_grouped, cols)
+
+        def fetch(t, cols):
+            nc.scalar.activation(b6[:, t, cols], win[t][:].indirect(offsets("n6", cols)), ACT.Copy)
+            nc.vector.tensor_tensor(
+                diff[:, t, cols], win[t][:].indirect(offsets("n7", cols)), b6[:, t, cols], ALU.subtract
+            )
+
+        def finish(t, cols):
+            nc.scalar.activation(gate[:, t, cols], diff[:, t, cols], ACT.Tanh, scale=-0.0625)
+            nc.vector.tensor_tensor(res[:, t, cols], gate[:, t, cols], a_ps[t][:, cols], ALU.mult)
+
+        def store(t):
+            nc.sync.dma_start(out=out_rows[:, t, :], in_=res[:, t, :])
+
+        for t in range(PACK - 1):
+            nc.scalar.copy(win[t][:, :S], b_ps[t][:])
+            fetch(t, whole)
+            if t > 0:
+                finish(t - 1, whole)
+                store(t - 1)
+        last = PACK - 1
+        nc.scalar.copy(win[last][:, :S], b_ps[last][:])
+        fetch(last, halves[0])
+        finish(last - 1, whole)
+        store(last - 1)
+        fetch(last, halves[1])
+        finish(last, halves[0])
+        interleave(nc, o_grouped, res, halves[0])
+        finish(last, halves[1])
+        store(last)
+        quantize(nc, o_w, o_s, o_grouped, halves[0])
+        interleave(nc, o_grouped, res, halves[1])
+        quantize(nc, o_w, o_s, o_grouped, halves[1])
         nc.sync.dma_start(out=out_1[0].rearrange("p n t -> p (n t)").bitcast(I32), in_=o_w[:])
         for k in range(4):
             queue = nc.scalar if k % 2 == 0 else nc.sync

@@ -18,12 +18,16 @@ ACT = mybir.ActivationFunctionType
 
 P = 128
 PACK = 4
+QUADRANTS = 4
+GROUP = 16
 WINDOW = 2 * S
 
 
-def load_scale_rows(queues, tile, rows):
-    for q, queue in enumerate(queues):
-        queue.dma_start(out=tile[32 * q : 32 * q + 4, :].bitcast(I32), in_=rows[0, 4 * q : 4 * q + 4, :].bitcast(I32))
+def load_scale_rows(queue, tile, rows):
+    for quad in range(QUADRANTS):
+        queue.dma_start(
+            out=tile[32 * quad : 32 * quad + 4, :].bitcast(I32), in_=rows[0, 4 * quad : 4 * quad + 4, :].bitcast(I32)
+        )
 
 
 def interleave(nc, grouped, planes, cols):
@@ -33,9 +37,9 @@ def interleave(nc, grouped, planes, cols):
     )
 
 
-def quantize(nc, codes, scales, grouped, cols):
+def quantize(nc, words, scales, grouped, cols):
     nc.vector.quantize_mx(
-        out=codes[:, cols].bitcast(FP8X4), scales=scales[:, cols], in_=grouped[:, cols, :].rearrange("p j t -> p (j t)")
+        out=words[:, cols].bitcast(FP8X4), scales=scales[:, cols], in_=grouped[:, cols, :].rearrange("p j t -> p (j t)")
     )
 
 
@@ -44,6 +48,10 @@ def tile_picked_fkcdjointbstdmix_none_po_kernel(
     offs, n1, n2, n3, n4, n5, cand, n6, n7, out_0, out_1, out_2,
 ):
     nc = tc.nc
+    last = PACK - 1
+    whole = slice(0, S)
+    halves = [slice(0, S // 2), slice(S // 2, S)]
+
     with ExitStack() as ctx:
         keep = ctx.enter_context(tc.tile_pool(name="keep", bufs=1))
         psum = ctx.enter_context(tc.psum_pool(name="psum", bufs=1))
@@ -59,51 +67,46 @@ def tile_picked_fkcdjointbstdmix_none_po_kernel(
         def load_list(name):
             nc.sync.dma_start(lists[name][0][:], lists[name][1])
 
-        def offsets(name, cols=slice(0, S)):
-            if name == "cand":
-                return lists[name][0][:]
-            return lists[name][0][:, cols.start // 16 : cols.stop // 16]
+        def offsets(name, entries):
+            return lists[name][0][:, entries.start // GROUP : entries.stop // GROUP]
 
-        xw = sb("xw", [P, T], I32)
-        xs = sb("xs", [P, T], U8)
-        w1w = sb("w1w", [P, 2 * K], U8)
-        w1s = sb("w1s", [P, K], U8)
-        w2w = sb("w2w", [P, 2 * K], U8)
-        w2s = sb("w2s", [P, K], U8)
+        x_w = sb("x_w", [P, T], I32)
+        x_s = sb("x_s", [P, T], U8)
+        w1_w = sb("w1_w", [P, 2 * K], U8)
+        w1_s = sb("w1_s", [P, K], U8)
+        w2_w = sb("w2_w", [P, 2 * K], U8)
+        w2_s = sb("w2_s", [P, K], U8)
         gn_sb = sb("gn_sb", [P, PACK], F32)
         gs_sb = sb("gs_sb", [P, PACK], F32)
-        win = [sb("win%d" % t, [P, WINDOW], F32) for t in range(PACK)]
+        window = [sb("window%d" % t, [P, WINDOW], F32) for t in range(PACK)]
 
-        nc.gpsimd.memset(w1s[:].bitcast(I32), 0)
-        nc.vector.memset(xs[:].bitcast(I32), 0)
+        nc.gpsimd.memset(w1_s[:].bitcast(I32), 0)
+        nc.vector.memset(x_s[:].bitcast(I32), 0)
         for t in range(PACK):
-            nc.vector.memset(win[t][:, S:], 0.0)
-        nc.vector.memset(w2s[:].bitcast(I32), 0)
+            nc.vector.memset(window[t][:, S:], 0.0)
+        nc.vector.memset(w2_s[:].bitcast(I32), 0)
 
         load_list("offs")
         load_list("cand")
-        nc.sync.dma_start(out=w1w[:].bitcast(I32), in_=w1_words[0].bitcast(I32))
-        nc.sync.dma_start(out=xw[:], in_=x_words[0].rearrange("p n t -> p (n t)").bitcast(I32))
-        load_scale_rows([nc.scalar] * 4, xs, x_scales)
-        load_scale_rows([nc.gpsimd, nc.gpsimd, nc.scalar, nc.scalar], w1s, w1_scales)
-        nc.gpsimd.dma_start(out=w2w[:].bitcast(I32), in_=w2_words[0].bitcast(I32))
-        load_list("n1")
-        load_list("n2")
-        load_list("n3")
-        load_list("n4")
-        load_list("n5")
-        load_scale_rows([nc.sync] * 4, w2s, w2_scales)
+        nc.sync.dma_start(out=w1_w[:].bitcast(I32), in_=w1_words[0].bitcast(I32))
+        nc.sync.dma_start(out=x_w[:], in_=x_words[0].rearrange("p n t -> p (n t)").bitcast(I32))
+        load_scale_rows(nc.scalar, x_s, x_scales)
+        load_scale_rows(nc.scalar, w1_s, w1_scales)
+        nc.gpsimd.dma_start(out=w2_w[:].bitcast(I32), in_=w2_words[0].bitcast(I32))
+        for name in ("n1", "n2", "n3", "n4", "n5"):
+            load_list(name)
+        load_scale_rows(nc.sync, w2_s, w2_scales)
         nc.sync.dma_start(out=gs_sb[:], in_=gs.rearrange("(p t) o -> p (t o)", t=PACK))
         nc.sync.dma_start(out=gn_sb[:], in_=gn.rearrange("(p t) o -> p (t o)", t=PACK))
         load_list("n6")
         load_list("n7")
 
-        unused = sb("unused", [P, 2], F32)
+        warm_up = sb("warm_up", [P, 2], F32)
         nc.scalar.activation(
-            unused[:, 0:1], win[0][:, S : S + 1], ACT.Abs_reciprocal_sqrt, bias=0.25, scale=0.5
+            warm_up[:, 0:1], window[0][:, S : S + 1], ACT.Abs_reciprocal_sqrt, bias=0.25, scale=0.5
         )
 
-        def deal_words(name, words):
+        def deal_fp4_words(name, words):
             dealt = sb(name, [P, 2 * K], U8)
             nc.scalar.copy(
                 out=dealt[:].bitcast(U16).rearrange("p (t m) -> p t m", t=PACK),
@@ -119,152 +122,156 @@ def tile_picked_fkcdjointbstdmix_none_po_kernel(
             )
             return dealt
 
-        w1_dw = deal_words("w1_dw", w1w)
-        w1_ds = deal("w1_ds", w1s, U8)
+        def fp4_product(banks, dealt_w, dealt_s, words, scales):
+            for t in range(PACK):
+                nc.tensor.matmul_mx(
+                    out=banks[t][:],
+                    lhsT=dealt_w[:, 2 * P * t : 2 * P * (t + 1)].bitcast(FP4X4),
+                    lhsT_scale=dealt_s[:, P * t : P * (t + 1)],
+                    rhs=words[:].bitcast(FP8X4),
+                    rhs_scale=scales[:],
+                    start=True,
+                    stop=True,
+                )
 
-        xq_w = sb("xq_w", [P, S], U32)
-        xq_s = sb("xq_s", [P, S], U8)
-        xc_w = sb("xc_w", [P, C], U32, tag="w1s")
-        xc_s = sb("xc_s", [P, C], U8, tag="xq_s")
-        nc.vector.tensor_copy(xq_s[:], xs[:].indirect(offsets("offs")))
-        nc.vector.tensor_copy(xq_w[:], xw[:].bitcast(U32).indirect(offsets("offs")))
+        w1_dealt_w = deal_fp4_words("w1_dealt_w", w1_w)
+        w1_dealt_s = deal("w1_dealt_s", w1_s, U8)
+
+        picked_w = sb("picked_w", [P, S], U32)
+        picked_s = sb("picked_s", [P, S], U8)
+        cand_w = sb("cand_w", [P, C], U32, tag="w1_s")
+        cand_s = sb("cand_s", [P, C], U8, tag="picked_s")
+        nc.vector.tensor_copy(picked_s[:], x_s[:].indirect(offsets("offs", whole)))
+        nc.vector.tensor_copy(picked_w[:], x_w[:].bitcast(U32).indirect(offsets("offs", whole)))
 
         y_ps = [psum.tile([P, S], F32, name="y_ps%d" % t, tag="low%d" % t) for t in range(PACK)]
-        for t in range(PACK):
-            nc.tensor.matmul_mx(
-                out=y_ps[t][:],
-                lhsT=w1_dw[:, 2 * P * t : 2 * P * (t + 1)].bitcast(FP4X4),
-                lhsT_scale=w1_ds[:, P * t : P * (t + 1)],
-                rhs=xq_w[:].bitcast(FP8X4),
-                rhs_scale=xq_s[:],
-                start=True,
-                stop=True,
-            )
+        fp4_product(y_ps, w1_dealt_w, w1_dealt_s, picked_w, picked_s)
 
-        w2_dw = deal_words("w2_dw", w2w)
-        nc.vector.tensor_copy(xc_w[:], xw[:].bitcast(U32).indirect(offsets("cand")))
-        nc.vector.tensor_copy(xc_s[:], xs[:].indirect(offsets("cand")))
-        xd_w = deal("xd_w", xc_w, U32)
-        xd_s = deal("xd_s", xc_s, U8)
-        w2_ds = deal("w2_ds", w2s, U8)
+        w2_dealt_w = deal_fp4_words("w2_dealt_w", w2_w)
+        nc.vector.tensor_copy(cand_w[:], x_w[:].bitcast(U32).indirect(offsets("cand", slice(0, C))))
+        nc.vector.tensor_copy(cand_s[:], x_s[:].indirect(offsets("cand", slice(0, C))))
+        cand_dealt_w = deal("cand_dealt_w", cand_w, U32)
+        cand_dealt_s = deal("cand_dealt_s", cand_s, U8)
+        w2_dealt_s = deal("w2_dealt_s", w2_s, U8)
         gn_scaled = sb("gn_scaled", [P, PACK], F32)
         nc.gpsimd.tensor_scalar(gn_scaled[:], gn_sb[:], 0.6875, 0.0, ALU.mult, ALU.add)
 
         pa = sb("pa", [P, PACK, S], F32)
         for t in range(PACK):
-            nc.scalar.copy(win[t][:, :S], y_ps[t][:])
-            nc.scalar.activation(pa[:, t, :], win[t][:].indirect(offsets("n1")), ACT.Copy)
+            nc.scalar.copy(window[t][:, :S], y_ps[t][:])
+            nc.scalar.activation(pa[:, t, :], window[t][:].indirect(offsets("n1", whole)), ACT.Copy)
 
         u = sb("u", [P, PACK, S], F32)
-        ev = sb("ev", [P, 2, 2, 2, S], F32)
-        dev = sb("dev", [P, PACK, S], F32)
+        spread = sb("spread", [P, 2, 2, 2, S], F32)
+        centred = sb("centred", [P, PACK, S], F32)
 
         def pair_sum(t):
-            nc.vector.tensor_tensor(u[:, t, :], win[t][:].indirect(offsets("n2")), pa[:, t, :], ALU.add)
+            nc.vector.tensor_tensor(u[:, t, :], window[t][:].indirect(offsets("n2", whole)), pa[:, t, :], ALU.add)
 
-        def spreads(t):
-            nc.vector.scalar_tensor_tensor(ev[:, t // 2, 1, t % 2, :], pa[:, t, :], -2.0, u[:, t, :], ALU.mult, ALU.add)
-            nc.vector.scalar_tensor_tensor(ev[:, t // 2, 0, t % 2, :], u[:, t, :], 0.6, y_ps[t][:], ALU.mult, ALU.subtract)
+        def spread_forms(t):
+            nc.vector.scalar_tensor_tensor(
+                spread[:, t // 2, 1, t % 2, :], pa[:, t, :], -2.0, u[:, t, :], ALU.mult, ALU.add
+            )
+            nc.vector.scalar_tensor_tensor(
+                spread[:, t // 2, 0, t % 2, :], u[:, t, :], 0.6, y_ps[t][:], ALU.mult, ALU.subtract
+            )
 
-        def deviation(t):
-            nc.vector.scalar_tensor_tensor(dev[:, t, :], u[:, t, :], -5.0 / 11.0, y_ps[t][:], ALU.mult, ALU.add)
+        def centre(t):
+            nc.vector.scalar_tensor_tensor(centred[:, t, :], u[:, t, :], -5.0 / 11.0, y_ps[t][:], ALU.mult, ALU.add)
 
         pair_sum(0)
-        pair_sum(1)
-        spreads(0)
-        pair_sum(2)
-        spreads(1)
-        pair_sum(3)
-        spreads(2)
-        spreads(3)
+        for t in range(1, PACK):
+            pair_sum(t)
+            spread_forms(t - 1)
+        spread_forms(last)
 
-        early = sb("early", [P, 2, 3, S], F32)
-        fetched = [[early[:, t, k, :] for k in range(3)] for t in range(2)]
-        fetched = fetched + [[ev[:, h, k // 2, k % 2, :] for k in range(3)] for h in range(2)]
-        m1 = sb("m1", [P, PACK, S], F32)
-        m2 = sb("m2", [P, PACK, S], F32)
-        dm = sb("dm", [P, PACK, S], F32)
+        fetched_low = sb("fetched_low", [P, 2, 3, S], F32)
+        fetched = [[fetched_low[:, t, k, :] for k in range(3)] for t in range(2)]
+        fetched = fetched + [[spread[:, pair, k // 2, k % 2, :] for k in range(3)] for pair in range(2)]
+        max_own = sb("max_own", [P, PACK, S], F32)
+        max_other = sb("max_other", [P, PACK, S], F32)
+        max_gap = sb("max_gap", [P, PACK, S], F32)
         z2_planes = sb("z2_planes", [P, PACK, S], BF16)
 
         def group_gathers(t, cols):
             for k, name in enumerate(("n3", "n4", "n5")):
-                nc.scalar.activation(fetched[t][k][:, cols], win[t][:].indirect(offsets(name, cols)), ACT.Copy)
+                nc.scalar.activation(fetched[t][k][:, cols], window[t][:].indirect(offsets(name, cols)), ACT.Copy)
 
         def maxima(t, cols):
-            nc.vector.tensor_tensor(m1[:, t, cols], fetched[t][0][:, cols], y_ps[t][:, cols], ALU.max)
-            nc.vector.tensor_tensor(m2[:, t, cols], fetched[t][1][:, cols], fetched[t][2][:, cols], ALU.max)
+            nc.vector.tensor_tensor(max_own[:, t, cols], fetched[t][0][:, cols], y_ps[t][:, cols], ALU.max)
+            nc.vector.tensor_tensor(max_other[:, t, cols], fetched[t][1][:, cols], fetched[t][2][:, cols], ALU.max)
 
         def max_difference(t, cols):
-            nc.vector.tensor_tensor(dm[:, t, cols], m1[:, t, cols], m2[:, t, cols], ALU.subtract)
+            nc.vector.tensor_tensor(max_gap[:, t, cols], max_own[:, t, cols], max_other[:, t, cols], ALU.subtract)
 
         def z2_round(t, cols):
-            nc.vector.tensor_scalar(z2_planes[:, t, cols], dm[:, t, cols], gs_sb[:, t : t + 1], None, ALU.mult)
+            nc.vector.tensor_scalar(z2_planes[:, t, cols], max_gap[:, t, cols], gs_sb[:, t : t + 1], None, ALU.mult)
 
-        sq = sb("sq", [P, 2, 2, 2 * S], F32)
-        q = sb("q", [P, 2, 2 * S], F32)
-        r = sb("r", [P, PACK, S], F32)
+        squared = sb("squared", [P, 2, 2, 2 * S], F32)
+        square_total = sb("square_total", [P, 2, 2 * S], F32)
+        inv_root = sb("inv_root", [P, PACK, S], F32)
 
-        def squares(h):
+        def squares(pair):
             nc.scalar.activation(
-                sq[:, h].rearrange("p k n -> p (k n)"), ev[:, h].rearrange("p k t n -> p (k t n)"), ACT.Square
+                squared[:, pair].rearrange("p k n -> p (k n)"),
+                spread[:, pair].rearrange("p k t n -> p (k t n)"),
+                ACT.Square,
             )
 
-        def square_sum(h):
-            nc.vector.scalar_tensor_tensor(q[:, h, :], sq[:, h, 0, :], 0.390625, sq[:, h, 1, :], ALU.mult, ALU.add)
+        def square_sum(pair):
+            nc.vector.scalar_tensor_tensor(
+                square_total[:, pair, :], squared[:, pair, 0, :], 0.625 * 0.625, squared[:, pair, 1, :],
+                ALU.mult, ALU.add,
+            )
 
-        whole = slice(0, S)
-        halves = [slice(0, S // 2), slice(S // 2, S)]
         group_gathers(0, whole)
         group_gathers(1, whole)
         squares(0)
         group_gathers(2, whole)
         squares(1)
         for cols in halves:
-            group_gathers(3, cols)
-        for t in range(3):
+            group_gathers(last, cols)
+        between = [lambda: centre(last), lambda: square_sum(0), lambda: square_sum(1)]
+        for t in range(last):
             maxima(t, whole)
-            deviation(t)
+            centre(t)
             max_difference(t, whole)
-            if t > 0:
-                square_sum(t - 1)
-            else:
-                deviation(3)
+            between[t]()
             z2_round(t, whole)
         nc.scalar.activation(
-            r[:].rearrange("p t n -> p (t n)"), q[:].rearrange("p h n -> p (h n)"), ACT.Abs_reciprocal_sqrt,
-            bias=0.25, scale=0.5,
+            inv_root[:].rearrange("p t n -> p (t n)"), square_total[:].rearrange("p h n -> p (h n)"),
+            ACT.Abs_reciprocal_sqrt, bias=0.25, scale=0.5,
         )
-
-        nc.scalar.activation(unused[:, 1:2], r[:, 0, 0:1], ACT.Tanh)
+        nc.scalar.activation(warm_up[:, 1:2], inv_root[:, 0, 0:1], ACT.Tanh)
 
         z2_grouped = sb("z2_grouped", [P, S, PACK], BF16)
         z2_w = sb("z2_w", [P, S], U32)
         z2_s = sb("z2_s", [P, S], U8)
-        b_ps = [psum.tile([P, S], F32, name="b_ps%d" % t, tag="high%d" % t) for t in range(PACK)]
+        scores_ps = [psum.tile([P, S], F32, name="scores_ps%d" % t, tag="high%d" % t) for t in range(PACK)]
         for cols in halves:
-            maxima(3, cols)
-            max_difference(3, cols)
-            z2_round(3, cols)
+            maxima(last, cols)
+            max_difference(last, cols)
+            z2_round(last, cols)
             interleave(nc, z2_grouped, z2_planes, cols)
             quantize(nc, z2_w, z2_s, z2_grouped, cols)
             for t in range(PACK):
                 nc.tensor.matmul_mx(
-                    out=b_ps[t][:, cols],
-                    lhsT=xd_w[:, P * t : P * (t + 1)].bitcast(FP8X4),
-                    lhsT_scale=xd_s[:, P * t : P * (t + 1)],
+                    out=scores_ps[t][:, cols],
+                    lhsT=cand_dealt_w[:, P * t : P * (t + 1)].bitcast(FP8X4),
+                    lhsT_scale=cand_dealt_s[:, P * t : P * (t + 1)],
                     rhs=z2_w[:, cols].bitcast(FP8X4),
                     rhs_scale=z2_s[:, cols],
                     start=True,
                     stop=True,
                 )
 
-        z_planes = sb("z_planes", [P, PACK, S], BF16)
+        z_planes = sb("z_planes", [P, PACK, S], BF16, tag="z2_planes")
         z_grouped = sb("z_grouped", [P, S, PACK], BF16)
         z_w = sb("z_w", [P, S], U32)
         z_s = sb("z_s", [P, S], U8)
         for t in range(PACK):
             nc.vector.scalar_tensor_tensor(
-                z_planes[:, t, :], dev[:, t, :], gn_scaled[:, t : t + 1], r[:, t, :], ALU.mult, ALU.mult
+                z_planes[:, t, :], centred[:, t, :], gn_scaled[:, t : t + 1], inv_root[:, t, :], ALU.mult, ALU.mult
             )
         for cols in halves:
             interleave(nc, z_grouped, z_planes, cols)
@@ -272,62 +279,55 @@ def tile_picked_fkcdjointbstdmix_none_po_kernel(
             quantize(nc, z_w, z_s, z_grouped, cols)
 
         a_ps = [psum.tile([P, S], F32, name="a_ps%d" % t, tag="low%d" % t) for t in range(PACK)]
-        for t in range(PACK):
-            nc.tensor.matmul_mx(
-                out=a_ps[t][:],
-                lhsT=w2_dw[:, 2 * P * t : 2 * P * (t + 1)].bitcast(FP4X4),
-                lhsT_scale=w2_ds[:, P * t : P * (t + 1)],
-                rhs=z_w[:].bitcast(FP8X4),
-                rhs_scale=z_s[:],
-                start=True,
-                stop=True,
-            )
+        fp4_product(a_ps, w2_dealt_w, w2_dealt_s, z_w, z_s)
 
-        b6 = sb("b6", [P, PACK, S], F32)
-        diff = sb("diff", [P, PACK, S], F32)
+        score_work = sb("score_work", [P, PACK + last, S], F32)
+        at_n6 = score_work[:, 0:PACK, :]
+        score_gap = score_work[:, last : PACK + last, :]
         gate = sb("gate", [P, PACK, S], F32)
-        res = sb("res", [P, PACK, S], F32)
-        out_rows = out_0.rearrange("(p t) j -> p t j", t=PACK)
+        result = sb("result", [P, PACK, S], F32)
+        out_planes = out_0.rearrange("(p t) j -> p t j", t=PACK)
+        out_grouped = sb("out_grouped", [P, S, PACK], BF16)
+        out_w = sb("out_w", [P, S], I32)
+        out_s = sb("out_s", [P, S], U8)
 
-        o_grouped = sb("o_grouped", [P, S, PACK], BF16)
-        o_w = sb("o_w", [P, S], I32)
-        o_s = sb("o_s", [P, S], U8)
+        def stage(t):
+            nc.scalar.copy(window[t][:, :S], scores_ps[t][:])
 
         def fetch(t, cols):
-            nc.scalar.activation(b6[:, t, cols], win[t][:].indirect(offsets("n6", cols)), ACT.Copy)
+            nc.scalar.activation(at_n6[:, t, cols], window[t][:].indirect(offsets("n6", cols)), ACT.Copy)
             nc.vector.tensor_tensor(
-                diff[:, t, cols], win[t][:].indirect(offsets("n7", cols)), b6[:, t, cols], ALU.subtract
+                score_gap[:, t, cols], window[t][:].indirect(offsets("n7", cols)), at_n6[:, t, cols], ALU.subtract
             )
 
         def finish(t, cols):
-            nc.scalar.activation(gate[:, t, cols], diff[:, t, cols], ACT.Tanh, scale=-0.0625)
-            nc.vector.tensor_tensor(res[:, t, cols], gate[:, t, cols], a_ps[t][:, cols], ALU.mult)
+            nc.scalar.activation(gate[:, t, cols], score_gap[:, t, cols], ACT.Tanh, scale=-0.0625)
+            nc.vector.tensor_tensor(result[:, t, cols], gate[:, t, cols], a_ps[t][:, cols], ALU.mult)
 
         def store(t):
-            nc.sync.dma_start(out=out_rows[:, t, :], in_=res[:, t, :])
+            nc.sync.dma_start(out=out_planes[:, t, :], in_=result[:, t, :])
 
-        for t in range(PACK - 1):
-            nc.scalar.copy(win[t][:, :S], b_ps[t][:])
+        stage(0)
+        for t in range(last):
+            stage(t + 1)
             fetch(t, whole)
-            if t > 0:
-                finish(t - 1, whole)
-                store(t - 1)
-        last = PACK - 1
-        nc.scalar.copy(win[last][:, :S], b_ps[last][:])
-        fetch(last, halves[0])
-        finish(last - 1, whole)
-        store(last - 1)
-        fetch(last, halves[1])
+        for t in range(last):
+            finish(t, whole)
+            store(t)
+            if t < len(halves):
+                fetch(last, halves[t])
         finish(last, halves[0])
-        interleave(nc, o_grouped, res, halves[0])
+        interleave(nc, out_grouped, result, halves[0])
         finish(last, halves[1])
         store(last)
-        quantize(nc, o_w, o_s, o_grouped, halves[0])
-        interleave(nc, o_grouped, res, halves[1])
-        quantize(nc, o_w, o_s, o_grouped, halves[1])
-        nc.sync.dma_start(out=out_1[0].rearrange("p n t -> p (n t)").bitcast(I32), in_=o_w[:])
-        for k in range(4):
-            queue = nc.scalar if k % 2 == 0 else nc.sync
+        quantize(nc, out_w, out_s, out_grouped, halves[0])
+        interleave(nc, out_grouped, result, halves[1])
+        quantize(nc, out_w, out_s, out_grouped, halves[1])
+
+        nc.sync.dma_start(out=out_1[0].rearrange("p n t -> p (n t)").bitcast(I32), in_=out_w[:])
+        for quad in range(QUADRANTS):
+            queue = nc.scalar if quad % 2 == 0 else nc.sync
             queue.dma_start(
-                out=out_2[0, 4 * k : 4 * k + 4, :].bitcast(I32), in_=o_s[32 * k : 32 * k + 4, :].bitcast(I32)
+                out=out_2[0, 4 * quad : 4 * quad + 4, :].bitcast(I32),
+                in_=out_s[32 * quad : 32 * quad + 4, :].bitcast(I32),
             )

from contextlib import ExitStack

import concourse.mybir as mybir

K, T, S, C = 512, 2048, 256, 512
FLOPS = 3 * 2 * 512 * 512 * 256

F32 = mybir.dt.float32
BF16 = mybir.dt.bfloat16
I32 = mybir.dt.int32
U32 = mybir.dt.uint32
U16 = mybir.dt.uint16
U8 = mybir.dt.uint8
FP8X4 = mybir.dt.float8_e4m3fn_x4
FP4X4 = mybir.dt.float4_e2m1fn_x4
ALU = mybir.AluOpType
ACT = mybir.ActivationFunctionType

P = 128
PACK = 4
QUADRANTS = 4
GROUP = 16
WINDOW = 2 * S


def load_scale_rows(queue, tile, rows):
    for quad in range(QUADRANTS):
        queue.dma_start(
            out=tile[32 * quad : 32 * quad + 4, :].bitcast(I32), in_=rows[0, 4 * quad : 4 * quad + 4, :].bitcast(I32)
        )


def interleave(nc, grouped, planes, cols):
    nc.vector.tensor_copy(
        out=grouped[:, cols, :].rearrange("p (c i) t -> p c t i", i=4),
        in_=planes[:, :, cols].rearrange("p t (c i) -> p c t i", i=4),
    )


def quantize(nc, words, scales, grouped, cols):
    nc.vector.quantize_mx(
        out=words[:, cols].bitcast(FP8X4), scales=scales[:, cols], in_=grouped[:, cols, :].rearrange("p j t -> p (j t)")
    )


def tile_picked_fkcdjointbstdmix_none_po_kernel(
    tc, x_words, x_scales, w1_words, w1_scales, gn, w2_words, w2_scales, gs,
    offs, n1, n2, n3, n4, n5, cand, n6, n7, out_0, out_1, out_2,
):
    nc = tc.nc
    last = PACK - 1
    whole = slice(0, S)
    halves = [slice(0, S // 2), slice(S // 2, S)]

    with ExitStack() as ctx:
        keep = ctx.enter_context(tc.tile_pool(name="keep", bufs=1))
        psum = ctx.enter_context(tc.psum_pool(name="psum", bufs=1))

        def sb(name, shape, dtype, tag=None):
            return keep.tile(shape, dtype, name=name, tag=tag or name, align_bytes=64)

        lists = {}
        for name, src in (("offs", offs), ("n1", n1), ("n2", n2), ("n3", n3), ("n4", n4), ("n5", n5),
                          ("cand", cand), ("n6", n6), ("n7", n7)):
            lists[name] = (sb("list_" + name, list(src.shape), U16), src)

        def load_list(name):
            nc.sync.dma_start(lists[name][0][:], lists[name][1])

        def offsets(name, entries):
            return lists[name][0][:, entries.start // GROUP : entries.stop // GROUP]

        x_w = sb("x_w", [P, T], I32)
        x_s = sb("x_s", [P, T], U8)
        w1_w = sb("w1_w", [P, 2 * K], U8)
        w1_s = sb("w1_s", [P, K], U8)
        w2_w = sb("w2_w", [P, 2 * K], U8)
        w2_s = sb("w2_s", [P, K], U8)
        gn_sb = sb("gn_sb", [P, PACK], F32)
        gs_sb = sb("gs_sb", [P, PACK], F32)
        window = [sb("window%d" % t, [P, WINDOW], F32) for t in range(PACK)]

        nc.gpsimd.memset(w1_s[:].bitcast(I32), 0)
        nc.vector.memset(x_s[:].bitcast(I32), 0)
        for t in range(PACK):
            nc.vector.memset(window[t][:, S:], 0.0)
        nc.vector.memset(w2_s[:].bitcast(I32), 0)

        load_list("offs")
        load_list("cand")
        nc.sync.dma_start(out=w1_w[:].bitcast(I32), in_=w1_words[0].bitcast(I32))
        nc.sync.dma_start(out=x_w[:], in_=x_words[0].rearrange("p n t -> p (n t)").bitcast(I32))
        load_scale_rows(nc.scalar, x_s, x_scales)
        load_scale_rows(nc.scalar, w1_s, w1_scales)
        nc.gpsimd.dma_start(out=w2_w[:].bitcast(I32), in_=w2_words[0].bitcast(I32))
        for name in ("n1", "n2", "n3", "n4", "n5"):
            load_list(name)
        load_scale_rows(nc.sync, w2_s, w2_scales)
        nc.sync.dma_start(out=gs_sb[:], in_=gs.rearrange("(p t) o -> p (t o)", t=PACK))
        nc.sync.dma_start(out=gn_sb[:], in_=gn.rearrange("(p t) o -> p (t o)", t=PACK))
        load_list("n6")
        load_list("n7")

        warm_up = sb("warm_up", [P, 2], F32)
        nc.scalar.activation(
            warm_up[:, 0:1], window[0][:, S : S + 1], ACT.Abs_reciprocal_sqrt, bias=0.25, scale=0.5
        )

        def deal_fp4_words(name, words):
            dealt = sb(name, [P, 2 * K], U8)
            nc.scalar.copy(
                out=dealt[:].bitcast(U16).rearrange("p (t m) -> p t m", t=PACK),
                in_=words[:].bitcast(U16).rearrange("p (m t) -> p t m", t=PACK),
            )
            return dealt

        def deal(name, columns, dtype):
            dealt = sb(name, [P, K], dtype)
            nc.vector.tensor_copy(
                out=dealt[:].rearrange("p (t m) -> p t m", t=PACK),
                in_=columns[:].rearrange("p (m t) -> p t m", t=PACK),
            )
            return dealt

        def fp4_product(banks, dealt_w, dealt_s, words, scales):
            for t in range(PACK):
                nc.tensor.matmul_mx(
                    out=banks[t][:],
                    lhsT=dealt_w[:, 2 * P * t : 2 * P * (t + 1)].bitcast(FP4X4),
                    lhsT_scale=dealt_s[:, P * t : P * (t + 1)],
                    rhs=words[:].bitcast(FP8X4),
                    rhs_scale=scales[:],
                    start=True,
                    stop=True,
                )

        w1_dealt_w = deal_fp4_words("w1_dealt_w", w1_w)
        w1_dealt_s = deal("w1_dealt_s", w1_s, U8)

        picked_w = sb("picked_w", [P, S], U32)
        picked_s = sb("picked_s", [P, S], U8)
        cand_w = sb("cand_w", [P, C], U32, tag="w1_s")
        cand_s = sb("cand_s", [P, C], U8, tag="picked_s")
        nc.vector.tensor_copy(picked_s[:], x_s[:].indirect(offsets("offs", whole)))
        nc.vector.tensor_copy(picked_w[:], x_w[:].bitcast(U32).indirect(offsets("offs", whole)))

        y_ps = [psum.tile([P, S], F32, name="y_ps%d" % t, tag="low%d" % t) for t in range(PACK)]
        fp4_product(y_ps, w1_dealt_w, w1_dealt_s, picked_w, picked_s)

        w2_dealt_w = deal_fp4_words("w2_dealt_w", w2_w)
        nc.vector.tensor_copy(cand_w[:], x_w[:].bitcast(U32).indirect(offsets("cand", slice(0, C))))
        nc.vector.tensor_copy(cand_s[:], x_s[:].indirect(offsets("cand", slice(0, C))))
        cand_dealt_w = deal("cand_dealt_w", cand_w, U32)
        cand_dealt_s = deal("cand_dealt_s", cand_s, U8)
        w2_dealt_s = deal("w2_dealt_s", w2_s, U8)
        gn_scaled = sb("gn_scaled", [P, PACK], F32)
        nc.gpsimd.tensor_scalar(gn_scaled[:], gn_sb[:], 0.6875, 0.0, ALU.mult, ALU.add)

        pa = sb("pa", [P, PACK, S], F32)
        for t in range(PACK):
            nc.scalar.copy(window[t][:, :S], y_ps[t][:])
            nc.scalar.activation(pa[:, t, :], window[t][:].indirect(offsets("n1", whole)), ACT.Copy)

        u = sb("u", [P, PACK, S], F32)
        spread = sb("spread", [P, 2, 2, 2, S], F32)
        centred = sb("centred", [P, PACK, S], F32)

        def pair_sum(t):
            nc.vector.tensor_tensor(u[:, t, :], window[t][:].indirect(offsets("n2", whole)), pa[:, t, :], ALU.add)

        def spread_forms(t):
            nc.vector.scalar_tensor_tensor(
                spread[:, t // 2, 1, t % 2, :], pa[:, t, :], -2.0, u[:, t, :], ALU.mult, ALU.add
            )
            nc.vector.scalar_tensor_tensor(
                spread[:, t // 2, 0, t % 2, :], u[:, t, :], 0.6, y_ps[t][:], ALU.mult, ALU.subtract
            )

        def centre(t):
            nc.vector.scalar_tensor_tensor(centred[:, t, :], u[:, t, :], -5.0 / 11.0, y_ps[t][:], ALU.mult, ALU.add)

        pair_sum(0)
        for t in range(1, PACK):
            pair_sum(t)
            spread_forms(t - 1)
        spread_forms(last)

        fetched_low = sb("fetched_low", [P, 2, 3, S], F32)
        fetched = [[fetched_low[:, t, k, :] for k in range(3)] for t in range(2)]
        fetched = fetched + [[spread[:, pair, k // 2, k % 2, :] for k in range(3)] for pair in range(2)]
        max_own = sb("max_own", [P, PACK, S], F32)
        max_other = sb("max_other", [P, PACK, S], F32)
        max_gap = sb("max_gap", [P, PACK, S], F32)
        z2_planes = sb("z2_planes", [P, PACK, S], BF16)

        def group_gathers(t, cols):
            for k, name in enumerate(("n3", "n4", "n5")):
                nc.scalar.activation(fetched[t][k][:, cols], window[t][:].indirect(offsets(name, cols)), ACT.Copy)

        def maxima(t, cols):
            nc.vector.tensor_tensor(max_own[:, t, cols], fetched[t][0][:, cols], y_ps[t][:, cols], ALU.max)
            nc.vector.tensor_tensor(max_other[:, t, cols], fetched[t][1][:, cols], fetched[t][2][:, cols], ALU.max)

        def max_difference(t, cols):
            nc.vector.tensor_tensor(max_gap[:, t, cols], max_own[:, t, cols], max_other[:, t, cols], ALU.subtract)

        def z2_round(t, cols):
            nc.vector.tensor_scalar(z2_planes[:, t, cols], max_gap[:, t, cols], gs_sb[:, t : t + 1], None, ALU.mult)

        squared = sb("squared", [P, 2, 2, 2 * S], F32)
        square_total = sb("square_total", [P, 2, 2 * S], F32)
        inv_root = sb("inv_root", [P, PACK, S], F32)

        def squares(pair):
            nc.scalar.activation(
                squared[:, pair].rearrange("p k n -> p (k n)"),
                spread[:, pair].rearrange("p k t n -> p (k t n)"),
                ACT.Square,
            )

        def square_sum(pair):
            nc.vector.scalar_tensor_tensor(
                square_total[:, pair, :], squared[:, pair, 0, :], 0.625 * 0.625, squared[:, pair, 1, :],
                ALU.mult, ALU.add,
            )

        group_gathers(0, whole)
        group_gathers(1, whole)
        squares(0)
        group_gathers(2, whole)
        squares(1)
        for cols in halves:
            group_gathers(last, cols)
        between = [lambda: centre(last), lambda: square_sum(0), lambda: square_sum(1)]
        for t in range(last):
            maxima(t, whole)
            centre(t)
            max_difference(t, whole)
            between[t]()
            z2_round(t, whole)
        nc.scalar.activation(
            inv_root[:].rearrange("p t n -> p (t n)"), square_total[:].rearrange("p h n -> p (h n)"),
            ACT.Abs_reciprocal_sqrt, bias=0.25, scale=0.5,
        )
        nc.scalar.activation(warm_up[:, 1:2], inv_root[:, 0, 0:1], ACT.Tanh)

        z2_grouped = sb("z2_grouped", [P, S, PACK], BF16)
        z2_w = sb("z2_w", [P, S], U32)
        z2_s = sb("z2_s", [P, S], U8)
        scores_ps = [psum.tile([P, S], F32, name="scores_ps%d" % t, tag="high%d" % t) for t in range(PACK)]
        for cols in halves:
            maxima(last, cols)
            max_difference(last, cols)
            z2_round(last, cols)
            interleave(nc, z2_grouped, z2_planes, cols)
            quantize(nc, z2_w, z2_s, z2_grouped, cols)
            for t in range(PACK):
                nc.tensor.matmul_mx(
                    out=scores_ps[t][:, cols],
                    lhsT=cand_dealt_w[:, P * t : P * (t + 1)].bitcast(FP8X4),
                    lhsT_scale=cand_dealt_s[:, P * t : P * (t + 1)],
                    rhs=z2_w[:, cols].bitcast(FP8X4),
                    rhs_scale=z2_s[:, cols],
                    start=True,
                    stop=True,
                )

        z_planes = sb("z_planes", [P, PACK, S], BF16, tag="z2_planes")
        z_grouped = sb("z_grouped", [P, S, PACK], BF16)
        z_w = sb("z_w", [P, S], U32)
        z_s = sb("z_s", [P, S], U8)
        for t in range(PACK):
            nc.vector.scalar_tensor_tensor(
                z_planes[:, t, :], centred[:, t, :], gn_scaled[:, t : t + 1], inv_root[:, t, :], ALU.mult, ALU.mult
            )
        for cols in halves:
            interleave(nc, z_grouped, z_planes, cols)
        for cols in halves:
            quantize(nc, z_w, z_s, z_grouped, cols)

        a_ps = [psum.tile([P, S], F32, name="a_ps%d" % t, tag="low%d" % t) for t in range(PACK)]
        fp4_product(a_ps, w2_dealt_w, w2_dealt_s, z_w, z_s)

        score_work = sb("score_work", [P, PACK + last, S], F32)
        at_n6 = score_work[:, 0:PACK, :]
        score_gap = score_work[:, last : PACK + last, :]
        gate = sb("gate", [P, PACK, S], F32)
        result = sb("result", [P, PACK, S], F32)
        out_planes = out_0.rearrange("(p t) j -> p t j", t=PACK)
        out_grouped = sb("out_grouped", [P, S, PACK], BF16)
        out_w = sb("out_w", [P, S], I32)
        out_s = sb("out_s", [P, S], U8)

        def stage(t):
            nc.scalar.copy(window[t][:, :S], scores_ps[t][:])

        def fetch(t, cols):
            nc.scalar.activation(at_n6[:, t, cols], window[t][:].indirect(offsets("n6", cols)), ACT.Copy)
            nc.vector.tensor_tensor(
                score_gap[:, t, cols], window[t][:].indirect(offsets("n7", cols)), at_n6[:, t, cols], ALU.subtract
            )

        def finish(t, cols):
            nc.scalar.activation(gate[:, t, cols], score_gap[:, t, cols], ACT.Tanh, scale=-0.0625)
            nc.vector.tensor_tensor(result[:, t, cols], gate[:, t, cols], a_ps[t][:, cols], ALU.mult)

        def store(t):
            nc.sync.dma_start(out=out_planes[:, t, :], in_=result[:, t, :])

        stage(0)
        for t in range(last):
            stage(t + 1)
            fetch(t, whole)
        for t in range(last):
            finish(t, whole)
            store(t)
            if t < len(halves):
                fetch(last, halves[t])
        finish(last, halves[0])
        interleave(nc, out_grouped, result, halves[0])
        finish(last, halves[1])
        store(last)
        quantize(nc, out_w, out_s, out_grouped, halves[0])
        interleave(nc, out_grouped, result, halves[1])
        quantize(nc, out_w, out_s, out_grouped, halves[1])

        nc.sync.dma_start(out=out_1[0].rearrange("p n t -> p (n t)").bitcast(I32), in_=out_w[:])
        for quad in range(QUADRANTS):
            queue = nc.scalar if quad % 2 == 0 else nc.sync
            queue.dma_start(
                out=out_2[0, 4 * quad : 4 * quad + 4, :].bitcast(I32),
                in_=out_s[32 * quad : 32 * quad + 4, :].bitcast(I32),
            )
